import numpy as np
import ml_dtypes


def mxq(x, axis, fmt="e4m3"):
    dtype, down = {"e4m3": (ml_dtypes.float8_e4m3fn, 7), "e5m2": (ml_dtypes.float8_e5m2, 14)}[fmt]
    v = np.moveaxis(np.asarray(x, np.float32).astype(ml_dtypes.bfloat16).astype(np.float64), axis, -1)
    blocks = v.reshape(v.shape[:-1] + (-1, 32))
    amax = np.abs(blocks).max(-1, keepdims=True)
    byte = np.maximum(np.where(amax > 0, np.frexp(amax)[1] - 1 + 127, 0) - down, 1)
    scale = np.exp2(byte - 127.0)
    codes = (blocks / scale).astype(np.float32).astype(dtype).astype(np.float64)
    return np.moveaxis((codes * scale).reshape(v.shape), -1, axis)


WIDE = False


def mx_kscale(k):
    if not WIDE:
        return np.ones(k)
    levels = np.array([10, -10, 5, -5, 0])
    if k % 512:
        return np.exp2(np.random.permutation(np.resize(levels, k // 32))).repeat(32)
    a = np.empty((k // 512, 16))
    for p in range(k // 512):
        a[p, :8] = np.random.permutation(np.resize(levels, 8))
        for g in range(8):
            far = levels[np.abs(levels - a[p, g]) >= 10]
            a[p, g + 8] = far[np.random.randint(len(far))]
    return np.exp2(a.ravel()).repeat(32)


def f64(x):
    return np.asarray(x).astype(np.float64)


def striped(idx):
    return np.tile(idx.reshape(-1, 16).T, (8, 1)).astype(np.uint16)


def unstriped(offs):
    return offs[:16].T.reshape(-1).astype(np.int64)


def striped8(idx):
    return np.concatenate([x.reshape(-1, 16).T for x in idx]).astype(np.uint16)


def runs(offs, k):
    lists = np.stack([offs[16 * r : 16 * r + 16].T.reshape(-1) for r in range(8)]).astype(np.int64)
    return lists[np.arange(k) % 512 // 64]


def pack_weight(w):
    k, n = w.shape
    w = f64(np.asarray(w, np.float32).astype(ml_dtypes.bfloat16)).reshape(k // 32, 32, n)
    amax = np.abs(w).max(1)
    byte = np.clip(np.where(amax > 0, np.frexp(amax)[1] - 1 + 127 - 7, 1), 1, 254)
    scaled = (w * np.exp2(127.0 - byte)[:, None, :]).reshape(k, n).astype(np.float32)
    words = np.ascontiguousarray(scaled.reshape(k // 512, 128, 4, n).transpose(0, 1, 3, 2)).astype(ml_dtypes.float8_e4m3fn).view(np.uint8)
    return words, np.ascontiguousarray(byte.astype(np.uint8).reshape(k // 512, 16, n))


def unpack_weight(words, scales):
    g, p, n, _ = words.shape
    vals = np.ascontiguousarray(words).view(ml_dtypes.float8_e4m3fn).astype(np.float64) * np.repeat(np.exp2(scales.astype(np.float64) - 127.0), 8, axis=1)[..., None]
    return vals.transpose(0, 1, 3, 2).reshape(g * 512, n)


def sigmoid(v):
    return 1.0 / (1.0 + np.exp(-np.maximum(v, -700.0)))


K, T, S, V, G, H = 512, 1024, 512, 512, 2048, 512


def setup_inputs():
    n = np.random.standard_normal
    s = mx_kscale(K)[:, None]
    u = mx_kscale(S)
    packed_xT = pack_weight(n((K, T)) * s)
    packed_dT = pack_weight(n((K, G)) / s)
    return {
        "x_words": packed_xT[0],
        "x_scales": packed_xT[1],
        "d_words": packed_dT[0],
        "d_scales": packed_dT[1],
        "w1": (n((K, H)) / np.sqrt(K) / s).astype(np.float32),
        "ga": (np.random.uniform(0.5, 1.5, (H, 1)) * u[:, None]).astype(np.float32),
        "gb": (np.random.uniform(0.5, 1.5, (H, 1)) / u[:, None]).astype(np.float32),
        "offs": striped(np.random.permutation(T)[:S]),
        "k1": striped8(np.random.randint(0, G, (8, H))),
        "two": striped(np.random.permutation(T)[:V]),
        "n1": striped8(np.stack([np.random.permutation(S) for _ in range(8)])),
        "n2": striped8(np.stack([np.random.permutation(S) for _ in range(8)])),
        "n3": striped8(np.stack([np.random.permutation(V) for _ in range(8)])),
        "n4": striped8(np.stack([np.random.permutation(V) for _ in range(8)])),
        "n5": striped8(np.stack([np.random.permutation(V) for _ in range(8)])),
        "n6": striped8(np.stack([np.random.permutation(V) for _ in range(8)])),
        "n7": striped8(np.stack([np.random.permutation(V) for _ in range(8)])),
    }


def reference(x_words, x_scales, d_words, d_scales, w1, ga, gb, offs, k1, two, n1, n2, n3, n4, n5, n6, n7):
    d_k1 = unpack_weight(d_words, d_scales)[np.arange(K)[:, None], runs(k1, K)]
    xq = unpack_weight(x_words, x_scales)[:, unstriped(offs)]
    a = 0.0625 * (d_k1.T @ xq)
    z = f64(ga) * (a[np.arange(H)[:, None], runs(n1, H)] - (a[np.arange(H)[:, None], runs(n2, H)]))
    x_two = unpack_weight(x_words, x_scales)[:, unstriped(two)]
    b = mxq(f64(w1), 0, "e4m3").T @ x_two
    pa = b[np.arange(H)[:, None], runs(n3, H)]
    z2 = f64(gb) * (pa + (sigmoid(b[np.arange(H)[:, None], runs(n4, H)])) * (b[np.arange(H)[:, None], runs(n5, H)] - pa))
    s = 0.0625 * ((mxq(z, 0, "e4m3").T @ mxq(z2, 0, "e4m3")))
    return np.maximum(s * (sigmoid(s[np.arange(S)[:, None], runs(n6, S)])), s[np.arange(S)[:, None], runs(n7, S)])

@@ -1,0 +1,247 @@
+from contextlib import ExitStack
+
+import concourse.mybir as mybir
+from concourse.masks import make_identity
+
+K, T, S, V, G, H = 512, 1024, 512, 512, 2048, 512
+FLOPS = 3 * 2 * 512 * 512 * 512
+
+F32 = mybir.dt.float32
+BF16 = mybir.dt.bfloat16
+I32 = mybir.dt.int32
+U32 = mybir.dt.uint32
+U16 = mybir.dt.uint16
+U8 = mybir.dt.uint8
+FP8X4 = mybir.dt.float8_e4m3fn_x4
+ACT = mybir.ActivationFunctionType
+ALU = mybir.AluOpType
+
+P = 128
+N = 512
+WIN = 1024
+
+
+def tile_picked_ckqgaplerpgmax_none_p_kernel(
+    tc, x_words, x_scales, d_words, d_scales, w1, ga, gb, offs, k1, two, n1, n2, n3, n4, n5, n6, n7, out
+):
+    nc = tc.nc
+    with ExitStack() as ctx:
+        keep = ctx.enter_context(tc.tile_pool(name="keep", bufs=1))
+        ring = ctx.enter_context(tc.tile_pool(name="ring", bufs=4))
+        psum = ctx.enter_context(tc.psum_pool(name="psum", bufs=1))
+
+        def load_list(name, src):
+            t = keep.tile([P, N // 16], U16, name=name)
+            nc.sync.dma_start(t[:], src)
+            return t
+
+        def mx(acc, lw, ls, rw, rs):
+            nc.tensor.matmul_mx(out=acc, lhsT=lw.bitcast(FP8X4), lhsT_scale=ls, rhs=rw.bitcast(FP8X4), rhs_scale=rs, start=True, stop=True)
+
+        xs = keep.tile([P, T], U8, name="xs")
+        nc.gpsimd.memset(xs[:].bitcast(I32), 0)
+        ds = keep.tile([P, G], U8, name="ds")
+        nc.gpsimd.memset(ds[:].bitcast(I32), 0)
+        warm = keep.tile([P, 1], F32, name="warm")
+        nc.vector.memset(warm[:], 0.0)
+        warm2 = keep.tile([P, 1], F32, name="warm2")
+        nc.scalar.activation(warm2[:], warm[:], ACT.Sigmoid)
+
+        l_two = load_list("l_two", two)
+        xw = keep.tile([P, T], U32, name="xw")
+        nc.sync.dma_start(xw[:].bitcast(I32), x_words[0].rearrange("p n t -> p (n t)").bitcast(I32))
+        for q in range(4):
+            nc.sync.dma_start(xs[32 * q : 32 * q + 4, :].bitcast(I32), x_scales[0, 4 * q : 4 * q + 4, :].bitcast(I32))
+        l_offs = load_list("l_offs", offs)
+        w_raw = []
+        for h in range(2):
+            wr = keep.tile([P, 4, H // 2], F32, name=f"w_raw{h}", tag=f"w_raw{h}", align_bytes=64)
+            nc.sync.dma_start(wr[:], w1.rearrange("(p j) c -> p j c", j=4)[:, :, h * 256 : (h + 1) * 256])
+            w_raw.append(wr)
+        for e in range(2):
+            nc.gpsimd.dma_start(ds[e:P:16, :].bitcast(I32), d_scales[0, e:16:2, :].bitcast(I32))
+        gb_t = keep.tile([P, 4], F32, name="gb_t")
+        nc.gpsimd.dma_start(gb_t[:], gb.rearrange("(p t) o -> p (t o)", t=4))
+        ga_t = keep.tile([P, 4], F32, name="ga_t")
+        nc.gpsimd.dma_start(ga_t[:], ga.rearrange("(p t) o -> p (t o)", t=4))
+        l_k1 = load_list("l_k1", k1)
+        l_n4 = load_list("l_n4", n4)
+        dw = keep.tile([P, G], U32, name="dw")
+        nc.sync.dma_start(dw[:].bitcast(I32), d_words[0].rearrange("p n t -> p (n t)").bitcast(I32))
+        l_n5 = load_list("l_n5", n5)
+        l_n3 = load_list("l_n3", n3)
+        l_n2 = load_list("l_n2", n2)
+        l_n1 = load_list("l_n1", n1)
+        l_n6 = load_list("l_n6", n6)
+        l_n7 = load_list("l_n7", n7)
+
+        ident = keep.tile([P, P], F32, name="ident")
+        make_identity(nc, ident[:])
+        ga16 = keep.tile([P, 4], F32, name="ga16")
+        nc.gpsimd.tensor_scalar(ga16[:], ga_t[:], 0.0625, 0.0, ALU.mult, ALU.add)
+        dsc = keep.tile([P, H], U8, name="dsc", align_bytes=64)
+        nc.gpsimd.memset(dsc[:].bitcast(I32), 0)
+
+        wb = keep.tile([P, 4 * H], BF16, name="wb", tag="wb", align_bytes=64)
+        wb_v = wb[:].rearrange("p (t m j) -> p m j t", t=4, j=4)
+        for h in range(2):
+            nc.scalar.copy(wb_v[:, 64 * h : 64 * (h + 1)], w_raw[h][:].rearrange("p j (m t) -> p m j t", t=4))
+
+        x2w = keep.tile([P, N], U32, name="x2w", align_bytes=64)
+        nc.vector.tensor_copy(x2w[:], xw[:].indirect(l_two[:]))
+        x2s = keep.tile([P, N], U8, name="x2s", align_bytes=64)
+        nc.vector.tensor_copy(x2s[:], xs[:].indirect(l_two[:]))
+        dgs = keep.tile([P, H], U8, name="dgs")
+        nc.vector.tensor_copy(dgs[:], ds[:].indirect(l_k1[:]))
+        x1s = keep.tile([P, N], U8, name="x1s", align_bytes=64)
+        nc.vector.tensor_copy(x1s[:], xs[:].indirect(l_offs[:]))
+        dds = keep.tile([P, H], U8, name="dds")
+        nc.vector.tensor_copy(dds[:].rearrange("p (t m) -> p m t", t=4), dgs[:].rearrange("p (m t) -> p m t", t=4))
+        for j, src in enumerate((0, 1, 16, 17)):
+            nc.sync.dma_start(dsc[j:P:32, :].bitcast(I32), dds[src:P:32, :].bitcast(I32))
+        ww = keep.tile([P, H], U32, name="ww", align_bytes=64)
+        ws = keep.tile([P, H], U8, name="ws", align_bytes=64)
+        nc.vector.quantize_mx(out=ww[:].bitcast(FP8X4), scales=ws[:], in_=wb[:])
+        dgw = keep.tile([P, H], U32, name="dgw", tag="wb", align_bytes=64)
+        nc.vector.tensor_copy(dgw[:], dw[:].indirect(l_k1[:]))
+        x1w = keep.tile([P, N], U32, name="x1w", tag="w_raw1", align_bytes=64)
+        nc.vector.tensor_copy(x1w[:], xw[:].indirect(l_offs[:]))
+
+        wins = [keep.tile([P, WIN], F32, name=f"win{i}") for i in range(12)]
+        zt_banks = [psum.tile([P, N], F32, name=f"zt{c}") for c in range(4)]
+        z = keep.tile([P, 4, N], F32, name="z")
+        state = {}
+
+        def b_raw(t):
+            acc = psum.tile([P, N], F32, name="acc", bufs=4)
+            mx(acc[:], ww[:, t * P : (t + 1) * P], ws[:, t * P : (t + 1) * P], x2w[:], x2s[:])
+            nc.scalar.copy(wins[8 + t][:, 0:N], acc[:])
+            state["acc", t] = acc
+
+        def b_gate(t):
+            nc.scalar.activation(wins[t][:, 0:N], state["acc", t][:], ACT.Copy, scale=gb_t[:, t : t + 1])
+            c5 = ring.tile([P, N], F32, name="sg")
+            nc.scalar.activation(c5[:], wins[8 + t][:].indirect(l_n4[:]), ACT.Sigmoid)
+            state["c5", t] = c5
+
+        def b_rest(t):
+            c3 = ring.tile([P, N], F32, name="c3")
+            nc.scalar.activation(c3[:], state["c5", t][:], ACT.Copy, bias=1.0, scale=-1.0)
+            state["c", t] = (state["c5", t], c3)
+
+        def b_back(t):
+            c5, c3 = state["c", t]
+            u = ring.tile([P, N], F32, name="u")
+            nc.vector.tensor_tensor(u[:], wins[t][:].indirect(l_n5[:]), c5[:], ALU.mult)
+            w = ring.tile([P, N], F32, name="w")
+            nc.vector.tensor_tensor(w[:], wins[t][:].indirect(l_n3[:]), c3[:], ALU.mult)
+            for c in range(4):
+                dst = zt_banks[c][:, t * P : (t + 1) * P]
+                nc.tensor.matmul(dst, u[:, c * P : (c + 1) * P], ident[:], start=True, stop=False, is_transpose=True)
+                nc.tensor.matmul(dst, w[:, c * P : (c + 1) * P], ident[:], start=False, stop=True, is_transpose=True)
+
+        ddw = keep.tile([P, H], U32, name="ddw", align_bytes=64)
+
+        def a_front(t):
+            acc = psum.tile([P, N], F32, name="acc", bufs=4)
+            mx(acc[:], ddw[:, t * P : (t + 1) * P], dsc[:, t * P : (t + 1) * P], x1w[:], x1s[:])
+            nc.scalar.activation(wins[4 + t][:, 0:N], acc[:], ACT.Copy, scale=ga16[:, t : t + 1])
+
+        def a_back(t):
+            g2 = keep.tile([P, N], F32, name=f"g2_{t}", tag="z2b" if t == 3 else f"g2_{t}", align_bytes=64)
+            nc.vector.tensor_copy(g2[:], wins[4 + t][:].indirect(l_n2[:]))
+            nc.vector.tensor_tensor(z[:, t, :], wins[4 + t][:].indirect(l_n1[:]), g2[:], ALU.subtract)
+
+        b_raw(0)
+        b_gate(0)
+        nc.vector.tensor_copy(ddw[:].rearrange("p (t m) -> p m t", t=4), dgw[:].rearrange("p (m t) -> p m t", t=4))
+        b_raw(1)
+        b_rest(0)
+        b_gate(1)
+        b_back(0)
+        b_raw(2)
+        b_rest(1)
+        b_back(1)
+        a_front(0)
+        b_gate(2)
+        a_back(0)
+        b_raw(3)
+        b_rest(2)
+        b_gate(3)
+        b_back(2)
+        a_front(1)
+        b_rest(3)
+        b_back(3)
+        a_front(2)
+        a_front(3)
+        a_back(1)
+
+        z2b = keep.tile([P, 4 * V], BF16, name="z2b", tag="z2b", align_bytes=64)
+        for pair in range(2):
+            back = psum.tile([P, N], F32, name="acc", bufs=4)
+            for c2 in range(2):
+                c = 2 * pair + c2
+                zr = ring.tile([P, N], BF16, name="zr")
+                nc.scalar.copy(zr[:].rearrange("v (u p e) -> v u p e", u=2, e=2), zt_banks[c][:].rearrange("v (u e p) -> v u p e", u=2, e=2))
+                words = zr[:].bitcast(F32)
+                for u in range(2):
+                    slot = 2 * c2 + u
+                    nc.tensor.transpose(back[:, slot * P : (slot + 1) * P], words[:, u * P : (u + 1) * P], ident[:])
+            nc.scalar.copy(
+                z2b[:].bitcast(F32)[:, pair * N : (pair + 1) * N].rearrange("p (c v u) -> p c v u", c=2, u=2),
+                back[:].rearrange("p (c u v) -> p c v u", c=2, u=2),
+            )
+        a_back(2)
+        z2w = keep.tile([P, V], U32, name="z2w", align_bytes=64)
+        z2s = keep.tile([P, V], U8, name="z2s", align_bytes=64)
+        nc.vector.quantize_mx(out=z2w[:].bitcast(FP8X4), scales=z2s[:], in_=z2b[:])
+        a_back(3)
+
+        z_v = z[:].rearrange("p h (g t u) -> p t g h u", t=4, u=4)
+        zbs = []
+        for t in range(4):
+            zb = keep.tile([P, N], BF16, name=f"zb{t}", align_bytes=64)
+            zbs.append(zb)
+
+        def z_round(t):
+            dst = zbs[t][:].rearrange("p (g u h) -> p g h u", u=4, h=4)
+            if t == 1:
+                nc.scalar.copy(dst, z_v[:, t])
+            else:
+                nc.vector.tensor_copy(dst, z_v[:, t])
+
+        def s_front(t):
+            zw = keep.tile([P, P], U32, name=f"zw{t}", align_bytes=64)
+            zs = keep.tile([P, P], U8, name=f"zs{t}", align_bytes=64)
+            nc.vector.quantize_mx(out=zw[:].bitcast(FP8X4), scales=zs[:], in_=zbs[t][:])
+            acc = psum.tile([P, N], F32, name="acc", bufs=4)
+            mx(acc[:], zw[:], zs[:], z2w[:], z2s[:])
+            nc.scalar.activation(wins[t][:, 0:N], acc[:], ACT.Copy, scale=0.0625)
+            sg = ring.tile([P, N], F32, name="sg")
+            nc.scalar.activation(sg[:], wins[t][:].indirect(l_n6[:]), ACT.Sigmoid)
+            state["s", t] = sg
+
+        z_round(0)
+        z_round(1)
+        z_round(2)
+        s_front(0)
+        z_round(3)
+        for t in range(1, 4):
+            s_front(t)
+
+        out_v = out.rearrange("(g t u) v -> t g u v", t=4, u=4)
+
+        def s_fetch(t):
+            g7 = ring.tile([P, N], F32, name="g7")
+            nc.vector.tensor_copy(g7[:], wins[t][:].indirect(l_n7[:]))
+            state["g", t] = g7
+
+        s_fetch(0)
+        for t in range(4):
+            m = ring.tile([P, N], F32, name="m")
+            nc.vector.tensor_tensor(m[:], wins[t][:, 0:N], state["s", t][:], ALU.mult)
+            if t < 3:
+                s_fetch(t + 1)
+            o = wins[(t + 1) % 4][:, N:WIN]
+            nc.vector.tensor_tensor(o, m[:], state["g", t][:], ALU.max)
+            nc.sync.dma_start(out_v[t], o)

@@ -28,6 +28,7 @@ def tile_picked_ckqgaplerpgmax_none_p_kernel(
     with ExitStack() as ctx:
         keep = ctx.enter_context(tc.tile_pool(name="keep", bufs=1))
         ring = ctx.enter_context(tc.tile_pool(name="ring", bufs=4))
+        shared = ctx.enter_context(tc.tile_pool(name="shared", bufs=1))
         psum = ctx.enter_context(tc.psum_pool(name="psum", bufs=1))
 
         def load_list(name, src):
@@ -39,35 +40,35 @@ def tile_picked_ckqgaplerpgmax_none_p_kernel(
             nc.tensor.matmul_mx(out=acc, lhsT=lw.bitcast(FP8X4), lhsT_scale=ls, rhs=rw.bitcast(FP8X4), rhs_scale=rs, start=True, stop=True)
 
         xs = keep.tile([P, T], U8, name="xs")
-        nc.gpsimd.memset(xs[:].bitcast(I32), 0)
         ds = keep.tile([P, G], U8, name="ds")
-        nc.gpsimd.memset(ds[:].bitcast(I32), 0)
         warm = keep.tile([P, 1], F32, name="warm")
         nc.vector.memset(warm[:], 0.0)
         warm2 = keep.tile([P, 1], F32, name="warm2")
         nc.scalar.activation(warm2[:], warm[:], ACT.Sigmoid)
 
         l_two = load_list("l_two", two)
+        xs_flat = x_scales[0].rearrange("q n -> (q n)")
+        for q in range(4):
+            nc.sync.dma_start(xs[32 * q : 32 * q + 32, :].bitcast(I32), xs_flat[4 * T * q : 4 * T * (q + 1)].bitcast(I32).partition_broadcast(8))
+        l_offs = load_list("l_offs", offs)
         xw = keep.tile([P, T], U32, name="xw")
         nc.sync.dma_start(xw[:].bitcast(I32), x_words[0].rearrange("p n t -> p (n t)").bitcast(I32))
-        for q in range(4):
-            nc.sync.dma_start(xs[32 * q : 32 * q + 4, :].bitcast(I32), x_scales[0, 4 * q : 4 * q + 4, :].bitcast(I32))
-        l_offs = load_list("l_offs", offs)
         w_raw = []
         for h in range(2):
             wr = keep.tile([P, 4, H // 2], F32, name=f"w_raw{h}", tag=f"w_raw{h}", align_bytes=64)
             nc.sync.dma_start(wr[:], w1.rearrange("(p j) c -> p j c", j=4)[:, :, h * 256 : (h + 1) * 256])
             w_raw.append(wr)
-        for e in range(2):
-            nc.gpsimd.dma_start(ds[e:P:16, :].bitcast(I32), d_scales[0, e:16:2, :].bitcast(I32))
+        nc.sync.dma_start(ds[:].bitcast(I32), d_scales[0].bitcast(I32).unsqueeze(1).to_broadcast([16, 8, G // 4]))
         gb_t = keep.tile([P, 4], F32, name="gb_t")
         nc.gpsimd.dma_start(gb_t[:], gb.rearrange("(p t) o -> p (t o)", t=4))
+        dsc = keep.tile([P, H], U8, name="dsc", align_bytes=64)
+        nc.gpsimd.memset(dsc[:].bitcast(I32), 0)
         ga_t = keep.tile([P, 4], F32, name="ga_t")
         nc.gpsimd.dma_start(ga_t[:], ga.rearrange("(p t) o -> p (t o)", t=4))
         l_k1 = load_list("l_k1", k1)
-        l_n4 = load_list("l_n4", n4)
         dw = keep.tile([P, G], U32, name="dw")
         nc.sync.dma_start(dw[:].bitcast(I32), d_words[0].rearrange("p n t -> p (n t)").bitcast(I32))
+        l_n4 = load_list("l_n4", n4)
         l_n5 = load_list("l_n5", n5)
         l_n3 = load_list("l_n3", n3)
         l_n2 = load_list("l_n2", n2)
@@ -79,49 +80,50 @@ def tile_picked_ckqgaplerpgmax_none_p_kernel(
         make_identity(nc, ident[:])
         ga16 = keep.tile([P, 4], F32, name="ga16")
         nc.gpsimd.tensor_scalar(ga16[:], ga_t[:], 0.0625, 0.0, ALU.mult, ALU.add)
-        dsc = keep.tile([P, H], U8, name="dsc", align_bytes=64)
-        nc.gpsimd.memset(dsc[:].bitcast(I32), 0)
 
-        wb = keep.tile([P, 4 * H], BF16, name="wb", tag="wb", align_bytes=64)
+        wb = shared.tile([P, 4 * H], BF16, name="wb", align_bytes=64, offset=0)
         wb_v = wb[:].rearrange("p (t m j) -> p m j t", t=4, j=4)
         for h in range(2):
             nc.scalar.copy(wb_v[:, 64 * h : 64 * (h + 1)], w_raw[h][:].rearrange("p j (m t) -> p m j t", t=4))
 
-        x2w = keep.tile([P, N], U32, name="x2w", align_bytes=64)
-        nc.vector.tensor_copy(x2w[:], xw[:].indirect(l_two[:]))
         x2s = keep.tile([P, N], U8, name="x2s", align_bytes=64)
         nc.vector.tensor_copy(x2s[:], xs[:].indirect(l_two[:]))
-        dgs = keep.tile([P, H], U8, name="dgs")
-        nc.vector.tensor_copy(dgs[:], ds[:].indirect(l_k1[:]))
         x1s = keep.tile([P, N], U8, name="x1s", align_bytes=64)
         nc.vector.tensor_copy(x1s[:], xs[:].indirect(l_offs[:]))
-        dds = keep.tile([P, H], U8, name="dds")
-        nc.vector.tensor_copy(dds[:].rearrange("p (t m) -> p m t", t=4), dgs[:].rearrange("p (m t) -> p m t", t=4))
-        for j, src in enumerate((0, 1, 16, 17)):
-            nc.sync.dma_start(dsc[j:P:32, :].bitcast(I32), dds[src:P:32, :].bitcast(I32))
+        x2w = keep.tile([P, N], U32, name="x2w", align_bytes=64)
+        nc.vector.tensor_copy(x2w[:], xw[:].indirect(l_two[:]))
+        x1w = keep.tile([P, N], U32, name="x1w", align_bytes=64)
+        nc.vector.tensor_copy(x1w[:], xw[:].indirect(l_offs[:]))
         ww = keep.tile([P, H], U32, name="ww", align_bytes=64)
         ws = keep.tile([P, H], U8, name="ws", align_bytes=64)
         nc.vector.quantize_mx(out=ww[:].bitcast(FP8X4), scales=ws[:], in_=wb[:])
-        dgw = keep.tile([P, H], U32, name="dgw", tag="wb", align_bytes=64)
+        dgs = shared.tile([P, H], U8, name="dgs", align_bytes=64, offset=0)
+        nc.vector.tensor_copy(dgs[:], ds[:].indirect(l_k1[:]))
+        dgw = shared.tile([P, H], U32, name="dgw", align_bytes=64, offset=2048)
+        dds = keep.tile([P, H], U8, name="dds")
+        nc.vector.tensor_copy(dds[:].rearrange("p (t m) -> p m t", t=4), dgs[:].rearrange("p (m t) -> p m t", t=4))
+        for j in range(4):
+            nc.sync.dma_start(dsc[j:P:32, :].bitcast(I32), dds[8 * j : P : 32, :].bitcast(I32))
         nc.vector.tensor_copy(dgw[:], dw[:].indirect(l_k1[:]))
-        x1w = keep.tile([P, N], U32, name="x1w", tag="w_raw1", align_bytes=64)
-        nc.vector.tensor_copy(x1w[:], xw[:].indirect(l_offs[:]))
 
-        wins = [keep.tile([P, WIN], F32, name=f"win{i}") for i in range(12)]
+        wins = [keep.tile([P, WIN], F32, name=f"win{i}") for i in range(4)]
+        raws = [keep.tile([P, WIN], F32, name=f"raw{i}") for i in range(4)]
+        awin = [raws[1], raws[3], raws[0], raws[2]]
         zt_banks = [psum.tile([P, N], F32, name=f"zt{c}") for c in range(4)]
-        z = keep.tile([P, 4, N], F32, name="z")
+        z5 = keep.tile([P, 5, N], F32, name="z5", align_bytes=64)
+        z = z5[:, 0:4, :]
         state = {}
 
         def b_raw(t):
             acc = psum.tile([P, N], F32, name="acc", bufs=4)
             mx(acc[:], ww[:, t * P : (t + 1) * P], ws[:, t * P : (t + 1) * P], x2w[:], x2s[:])
-            nc.scalar.copy(wins[8 + t][:, 0:N], acc[:])
+            nc.scalar.copy(raws[t][:, 0:N], acc[:])
             state["acc", t] = acc
 
         def b_gate(t):
             nc.scalar.activation(wins[t][:, 0:N], state["acc", t][:], ACT.Copy, scale=gb_t[:, t : t + 1])
             c5 = ring.tile([P, N], F32, name="sg")
-            nc.scalar.activation(c5[:], wins[8 + t][:].indirect(l_n4[:]), ACT.Sigmoid)
+            nc.scalar.activation(c5[:], raws[t][:].indirect(l_n4[:]), ACT.Sigmoid)
             state["c5", t] = c5
 
         def b_rest(t):
@@ -135,6 +137,7 @@ def tile_picked_ckqgaplerpgmax_none_p_kernel(
             nc.vector.tensor_tensor(u[:], wins[t][:].indirect(l_n5[:]), c5[:], ALU.mult)
             w = ring.tile([P, N], F32, name="w")
             nc.vector.tensor_tensor(w[:], wins[t][:].indirect(l_n3[:]), c3[:], ALU.mult)
+            state["u", t] = u
             for c in range(4):
                 dst = zt_banks[c][:, t * P : (t + 1) * P]
                 nc.tensor.matmul(dst, u[:, c * P : (c + 1) * P], ident[:], start=True, stop=False, is_transpose=True)
@@ -142,29 +145,41 @@ def tile_picked_ckqgaplerpgmax_none_p_kernel(
 
         ddw = keep.tile([P, H], U32, name="ddw", align_bytes=64)
 
-        def a_front(t):
+        def a_mm(t):
             acc = psum.tile([P, N], F32, name="acc", bufs=4)
             mx(acc[:], ddw[:, t * P : (t + 1) * P], dsc[:, t * P : (t + 1) * P], x1w[:], x1s[:])
-            nc.scalar.activation(wins[4 + t][:, 0:N], acc[:], ACT.Copy, scale=ga16[:, t : t + 1])
+            state["aacc", t] = acc
 
-        def a_back(t):
-            g2 = keep.tile([P, N], F32, name=f"g2_{t}", tag="z2b" if t == 3 else f"g2_{t}", align_bytes=64)
-            nc.vector.tensor_copy(g2[:], wins[4 + t][:].indirect(l_n2[:]))
-            nc.vector.tensor_tensor(z[:, t, :], wins[4 + t][:].indirect(l_n1[:]), g2[:], ALU.subtract)
+        def a_out(t):
+            nc.scalar.activation(awin[t][:, 0:N], state["aacc", t][:], ACT.Copy, scale=ga16[:, t : t + 1])
 
+        def a_front(t):
+            a_mm(t)
+            a_out(t)
+
+        def a_fetch(t, g2):
+            nc.vector.tensor_copy(g2, awin[t][:].indirect(l_n2[:]))
+            state["g2", t] = g2
+
+        def a_sub(t):
+            nc.vector.tensor_tensor(z5[:, t, :], awin[t][:].indirect(l_n1[:]), state["g2", t], ALU.subtract)
+
+        g2a = keep.tile([P, N], F32, name="g2a")
         b_raw(0)
         b_gate(0)
         nc.vector.tensor_copy(ddw[:].rearrange("p (t m) -> p m t", t=4), dgw[:].rearrange("p (m t) -> p m t", t=4))
         b_raw(1)
         b_rest(0)
+        a_mm(0)
         b_gate(1)
         b_back(0)
+        a_out(0)
         b_raw(2)
         b_rest(1)
         b_back(1)
-        a_front(0)
+        a_fetch(0, g2a[:])
+        a_sub(0)
         b_gate(2)
-        a_back(0)
         b_raw(3)
         b_rest(2)
         b_gate(3)
@@ -174,9 +189,12 @@ def tile_picked_ckqgaplerpgmax_none_p_kernel(
         b_back(3)
         a_front(2)
         a_front(3)
-        a_back(1)
+        a_fetch(1, state["c", 3][1][:])
+        a_fetch(2, wins[3][:, N:WIN])
+        a_sub(1)
+        a_fetch(3, state["u", 3][:])
+        a_sub(2)
 
-        z2b = keep.tile([P, 4 * V], BF16, name="z2b", tag="z2b", align_bytes=64)
         for pair in range(2):
             back = psum.tile([P, N], F32, name="acc", bufs=4)
             for c2 in range(2):
@@ -188,16 +206,17 @@ def tile_picked_ckqgaplerpgmax_none_p_kernel(
                     slot = 2 * c2 + u
                     nc.tensor.transpose(back[:, slot * P : (slot + 1) * P], words[:, u * P : (u + 1) * P], ident[:])
             nc.scalar.copy(
-                z2b[:].bitcast(F32)[:, pair * N : (pair + 1) * N].rearrange("p (c v u) -> p c v u", c=2, u=2),
+                z5[:, 4 - pair, :].rearrange("p (c v u) -> p c v u", c=2, u=2),
                 back[:].rearrange("p (c u v) -> p c v u", c=2, u=2),
             )
-        a_back(2)
         z2w = keep.tile([P, V], U32, name="z2w", align_bytes=64)
         z2s = keep.tile([P, V], U8, name="z2s", align_bytes=64)
-        nc.vector.quantize_mx(out=z2w[:].bitcast(FP8X4), scales=z2s[:], in_=z2b[:])
-        a_back(3)
+        for pair in range(2):
+            cols = slice(pair * 256, (pair + 1) * 256)
+            nc.vector.quantize_mx(out=z2w[:, cols].bitcast(FP8X4), scales=z2s[:, cols], in_=z5[:, 4 - pair, :].bitcast(BF16))
+        a_sub(3)
 
-        z_v = z[:].rearrange("p h (g t u) -> p t g h u", t=4, u=4)
+        z_v = z.rearrange("p h (g t u) -> p t g h u", t=4, u=4)
         zbs = []
         for t in range(4):
             zb = keep.tile([P, N], BF16, name=f"zb{t}", align_bytes=64)
@@ -239,9 +258,12 @@ def tile_picked_ckqgaplerpgmax_none_p_kernel(
         s_fetch(0)
         for t in range(4):
             m = ring.tile([P, N], F32, name="m")
-            nc.vector.tensor_tensor(m[:], wins[t][:, 0:N], state["s", t][:], ALU.mult)
+            o = wins[(t + 1) % 4][:, N:WIN]
+            parts = [slice(0, N)] if t < 3 else [slice(0, N // 2), slice(N // 2, N)]
+            for cols in parts:
+                nc.vector.tensor_tensor(m[:, cols], wins[t][:, cols], state["s", t][:, cols], ALU.mult)
             if t < 3:
                 s_fetch(t + 1)
-            o = wins[(t + 1) % 4][:, N:WIN]
-            nc.vector.tensor_tensor(o, m[:], state["g", t][:], ALU.max)
-            nc.sync.dma_start(out_v[t], o)
+            for cols in parts:
+                nc.vector.tensor_tensor(o[:, cols], m[:, cols], state["g", t][:, cols], ALU.max)
+                nc.sync.dma_start(out_v[t][:, :, cols], o[:, cols])

@@ -114,11 +114,13 @@ def tile_picked_ckqgaplerpgmax_none_p_kernel(
         z = z5[:, 0:4, :]
         state = {}
 
-        def b_raw(t):
+        def b_mm(t):
             acc = psum.tile([P, N], F32, name="acc", bufs=4)
             mx(acc[:], ww[:, t * P : (t + 1) * P], ws[:, t * P : (t + 1) * P], x2w[:], x2s[:])
-            nc.scalar.copy(raws[t][:, 0:N], acc[:])
             state["acc", t] = acc
+
+        def b_raw(t):
+            nc.scalar.copy(raws[t][:, 0:N], state["acc", t][:])
 
         def b_gate(t):
             nc.scalar.activation(wins[t][:, 0:N], state["acc", t][:], ACT.Copy, scale=gb_t[:, t : t + 1])
@@ -153,9 +155,6 @@ def tile_picked_ckqgaplerpgmax_none_p_kernel(
         def a_out(t):
             nc.scalar.activation(awin[t][:, 0:N], state["aacc", t][:], ACT.Copy, scale=ga16[:, t : t + 1])
 
-        def a_front(t):
-            a_mm(t)
-            a_out(t)
 
         def a_fetch(t, g2):
             nc.vector.tensor_copy(g2, awin[t][:].indirect(l_n2[:]))
@@ -165,6 +164,8 @@ def tile_picked_ckqgaplerpgmax_none_p_kernel(
             nc.vector.tensor_tensor(z5[:, t, :], awin[t][:].indirect(l_n1[:]), state["g2", t], ALU.subtract)
 
         g2a = keep.tile([P, N], F32, name="g2a")
+        for t in range(4):
+            b_mm(t)
         b_raw(0)
         b_gate(0)
         nc.vector.tensor_copy(ddw[:].rearrange("p (t m) -> p m t", t=4), dgw[:].rearrange("p (m t) -> p m t", t=4))
@@ -172,23 +173,26 @@ def tile_picked_ckqgaplerpgmax_none_p_kernel(
         b_rest(0)
         a_mm(0)
         b_gate(1)
+        a_mm(1)
         b_back(0)
         a_out(0)
         b_raw(2)
         b_rest(1)
+        b_gate(2)
+        a_mm(2)
         b_back(1)
         a_fetch(0, g2a[:])
         a_sub(0)
-        b_gate(2)
         b_raw(3)
         b_rest(2)
         b_gate(3)
+        a_mm(3)
         b_back(2)
-        a_front(1)
+        a_out(1)
         b_rest(3)
         b_back(3)
-        a_front(2)
-        a_front(3)
+        a_out(2)
+        a_out(3)
         a_fetch(1, state["c", 3][1][:])
         a_fetch(2, wins[3][:, N:WIN])
         a_sub(1)
@@ -224,7 +228,7 @@ def tile_picked_ckqgaplerpgmax_none_p_kernel(
 
         def z_round(t):
             dst = zbs[t][:].rearrange("p (g u h) -> p g h u", u=4, h=4)
-            if t == 1:
+            if t in (1, 2):
                 nc.scalar.copy(dst, z_v[:, t])
             else:
                 nc.vector.tensor_copy(dst, z_v[:, t])
@@ -243,9 +247,8 @@ def tile_picked_ckqgaplerpgmax_none_p_kernel(
         z_round(0)
         z_round(1)
         z_round(2)
-        s_front(0)
         z_round(3)
-        for t in range(1, 4):
+        for t in range(4):
             s_front(t)
 
         out_v = out.rearrange("(g t u) v -> t g u v", t=4, u=4)

from contextlib import ExitStack

import concourse.mybir as mybir
from concourse.masks import make_identity

K, T, S, V, G, H = 512, 1024, 512, 512, 2048, 512
FLOPS = 3 * 2 * 512 * 512 * 512

F32 = mybir.dt.float32
BF16 = mybir.dt.bfloat16
I32 = mybir.dt.int32
U32 = mybir.dt.uint32
U16 = mybir.dt.uint16
U8 = mybir.dt.uint8
FP8X4 = mybir.dt.float8_e4m3fn_x4
ACT = mybir.ActivationFunctionType
ALU = mybir.AluOpType

P = 128
N = 512
WIN = 1024


def tile_picked_ckqgaplerpgmax_none_p_kernel(
    tc, x_words, x_scales, d_words, d_scales, w1, ga, gb, offs, k1, two, n1, n2, n3, n4, n5, n6, n7, out
):
    nc = tc.nc
    with ExitStack() as ctx:
        keep = ctx.enter_context(tc.tile_pool(name="keep", bufs=1))
        ring = ctx.enter_context(tc.tile_pool(name="ring", bufs=4))
        shared = ctx.enter_context(tc.tile_pool(name="shared", bufs=1))
        psum = ctx.enter_context(tc.psum_pool(name="psum", bufs=1))

        def load_list(name, src):
            t = keep.tile([P, N // 16], U16, name=name)
            nc.sync.dma_start(t[:], src)
            return t

        def mx(acc, lw, ls, rw, rs):
            nc.tensor.matmul_mx(out=acc, lhsT=lw.bitcast(FP8X4), lhsT_scale=ls, rhs=rw.bitcast(FP8X4), rhs_scale=rs, start=True, stop=True)

        xs = keep.tile([P, T], U8, name="xs")
        ds = keep.tile([P, G], U8, name="ds")
        warm = keep.tile([P, 1], F32, name="warm")
        nc.vector.memset(warm[:], 0.0)
        warm2 = keep.tile([P, 1], F32, name="warm2")
        nc.scalar.activation(warm2[:], warm[:], ACT.Sigmoid)

        l_two = load_list("l_two", two)
        xs_flat = x_scales[0].rearrange("q n -> (q n)")
        for q in range(4):
            nc.sync.dma_start(xs[32 * q : 32 * q + 32, :].bitcast(I32), xs_flat[4 * T * q : 4 * T * (q + 1)].bitcast(I32).partition_broadcast(8))
        l_offs = load_list("l_offs", offs)
        xw = keep.tile([P, T], U32, name="xw")
        nc.sync.dma_start(xw[:].bitcast(I32), x_words[0].rearrange("p n t -> p (n t)").bitcast(I32))
        w_raw = []
        for h in range(2):
            wr = keep.tile([P, 4, H // 2], F32, name=f"w_raw{h}", tag=f"w_raw{h}", align_bytes=64)
            nc.sync.dma_start(wr[:], w1.rearrange("(p j) c -> p j c", j=4)[:, :, h * 256 : (h + 1) * 256])
            w_raw.append(wr)
        nc.sync.dma_start(ds[:].bitcast(I32), d_scales[0].bitcast(I32).unsqueeze(1).to_broadcast([16, 8, G // 4]))
        gb_t = keep.tile([P, 4], F32, name="gb_t")
        nc.gpsimd.dma_start(gb_t[:], gb.rearrange("(p t) o -> p (t o)", t=4))
        dsc = keep.tile([P, H], U8, name="dsc", align_bytes=64)
        nc.gpsimd.memset(dsc[:].bitcast(I32), 0)
        ga_t = keep.tile([P, 4], F32, name="ga_t")
        nc.gpsimd.dma_start(ga_t[:], ga.rearrange("(p t) o -> p (t o)", t=4))
        l_k1 = load_list("l_k1", k1)
        dw = keep.tile([P, G], U32, name="dw")
        nc.sync.dma_start(dw[:].bitcast(I32), d_words[0].rearrange("p n t -> p (n t)").bitcast(I32))
        l_n4 = load_list("l_n4", n4)
        l_n5 = load_list("l_n5", n5)
        l_n3 = load_list("l_n3", n3)
        l_n2 = load_list("l_n2", n2)
        l_n1 = load_list("l_n1", n1)
        l_n6 = load_list("l_n6", n6)
        l_n7 = load_list("l_n7", n7)

        ident = keep.tile([P, P], F32, name="ident")
        make_identity(nc, ident[:])
        ga16 = keep.tile([P, 4], F32, name="ga16")
        nc.gpsimd.tensor_scalar(ga16[:], ga_t[:], 0.0625, 0.0, ALU.mult, ALU.add)

        wb = shared.tile([P, 4 * H], BF16, name="wb", align_bytes=64, offset=0)
        wb_v = wb[:].rearrange("p (t m j) -> p m j t", t=4, j=4)
        for h in range(2):
            nc.scalar.copy(wb_v[:, 64 * h : 64 * (h + 1)], w_raw[h][:].rearrange("p j (m t) -> p m j t", t=4))

        x2s = keep.tile([P, N], U8, name="x2s", align_bytes=64)
        nc.vector.tensor_copy(x2s[:], xs[:].indirect(l_two[:]))
        x1s = keep.tile([P, N], U8, name="x1s", align_bytes=64)
        nc.vector.tensor_copy(x1s[:], xs[:].indirect(l_offs[:]))
        x2w = keep.tile([P, N], U32, name="x2w", align_bytes=64)
        nc.vector.tensor_copy(x2w[:], xw[:].indirect(l_two[:]))
        x1w = keep.tile([P, N], U32, name="x1w", align_bytes=64)
        nc.vector.tensor_copy(x1w[:], xw[:].indirect(l_offs[:]))
        ww = keep.tile([P, H], U32, name="ww", align_bytes=64)
        ws = keep.tile([P, H], U8, name="ws", align_bytes=64)
        nc.vector.quantize_mx(out=ww[:].bitcast(FP8X4), scales=ws[:], in_=wb[:])
        dgs = shared.tile([P, H], U8, name="dgs", align_bytes=64, offset=0)
        nc.vector.tensor_copy(dgs[:], ds[:].indirect(l_k1[:]))
        dgw = shared.tile([P, H], U32, name="dgw", align_bytes=64, offset=2048)
        dds = keep.tile([P, H], U8, name="dds")
        nc.vector.tensor_copy(dds[:].rearrange("p (t m) -> p m t", t=4), dgs[:].rearrange("p (m t) -> p m t", t=4))
        for j in range(4):
            nc.sync.dma_start(dsc[j:P:32, :].bitcast(I32), dds[8 * j : P : 32, :].bitcast(I32))
        nc.vector.tensor_copy(dgw[:], dw[:].indirect(l_k1[:]))

        wins = [keep.tile([P, WIN], F32, name=f"win{i}") for i in range(4)]
        raws = [keep.tile([P, WIN], F32, name=f"raw{i}") for i in range(4)]
        awin = [raws[1], raws[3], raws[0], raws[2]]
        zt_banks = [psum.tile([P, N], F32, name=f"zt{c}") for c in range(4)]
        z5 = keep.tile([P, 5, N], F32, name="z5", align_bytes=64)
        z = z5[:, 0:4, :]
        state = {}

        def b_mm(t):
            acc = psum.tile([P, N], F32, name="acc", bufs=4)
            mx(acc[:], ww[:, t * P : (t + 1) * P], ws[:, t * P : (t + 1) * P], x2w[:], x2s[:])
            state["acc", t] = acc

        def b_raw(t):
            nc.scalar.copy(raws[t][:, 0:N], state["acc", t][:])

        def b_gate(t):
            nc.scalar.activation(wins[t][:, 0:N], state["acc", t][:], ACT.Copy, scale=gb_t[:, t : t + 1])
            c5 = ring.tile([P, N], F32, name="sg")
            nc.scalar.activation(c5[:], raws[t][:].indirect(l_n4[:]), ACT.Sigmoid)
            state["c5", t] = c5

        def b_rest(t):
            c3 = ring.tile([P, N], F32, name="c3")
            nc.scalar.activation(c3[:], state["c5", t][:], ACT.Copy, bias=1.0, scale=-1.0)
            state["c", t] = (state["c5", t], c3)

        def b_back(t):
            c5, c3 = state["c", t]
            u = ring.tile([P, N], F32, name="u")
            nc.vector.tensor_tensor(u[:], wins[t][:].indirect(l_n5[:]), c5[:], ALU.mult)
            w = ring.tile([P, N], F32, name="w")
            nc.vector.tensor_tensor(w[:], wins[t][:].indirect(l_n3[:]), c3[:], ALU.mult)
            state["u", t] = u
            for c in range(4):
                dst = zt_banks[c][:, t * P : (t + 1) * P]
                nc.tensor.matmul(dst, u[:, c * P : (c + 1) * P], ident[:], start=True, stop=False, is_transpose=True)
                nc.tensor.matmul(dst, w[:, c * P : (c + 1) * P], ident[:], start=False, stop=True, is_transpose=True)

        ddw = keep.tile([P, H], U32, name="ddw", align_bytes=64)

        def a_mm(t):
            acc = psum.tile([P, N], F32, name="acc", bufs=4)
            mx(acc[:], ddw[:, t * P : (t + 1) * P], dsc[:, t * P : (t + 1) * P], x1w[:], x1s[:])
            state["aacc", t] = acc

        def a_out(t):
            nc.scalar.activation(awin[t][:, 0:N], state["aacc", t][:], ACT.Copy, scale=ga16[:, t : t + 1])


        def a_fetch(t, g2):
            nc.vector.tensor_copy(g2, awin[t][:].indirect(l_n2[:]))
            state["g2", t] = g2

        def a_sub(t):
            nc.vector.tensor_tensor(z5[:, t, :], awin[t][:].indirect(l_n1[:]), state["g2", t], ALU.subtract)

        g2a = keep.tile([P, N], F32, name="g2a")
        for t in range(4):
            b_mm(t)
        b_raw(0)
        b_gate(0)
        nc.vector.tensor_copy(ddw[:].rearrange("p (t m) -> p m t", t=4), dgw[:].rearrange("p (m t) -> p m t", t=4))
        b_raw(1)
        b_rest(0)
        a_mm(0)
        b_gate(1)
        a_mm(1)
        b_back(0)
        a_out(0)
        b_raw(2)
        b_rest(1)
        b_gate(2)
        a_mm(2)
        b_back(1)
        a_fetch(0, g2a[:])
        a_sub(0)
        b_raw(3)
        b_rest(2)
        b_gate(3)
        a_mm(3)
        b_back(2)
        a_out(1)
        b_rest(3)
        b_back(3)
        a_out(2)
        a_out(3)
        a_fetch(1, state["c", 3][1][:])
        a_fetch(2, wins[3][:, N:WIN])
        a_sub(1)
        a_fetch(3, state["u", 3][:])
        a_sub(2)

        for pair in range(2):
            back = psum.tile([P, N], F32, name="acc", bufs=4)
            for c2 in range(2):
                c = 2 * pair + c2
                zr = ring.tile([P, N], BF16, name="zr")
                nc.scalar.copy(zr[:].rearrange("v (u p e) -> v u p e", u=2, e=2), zt_banks[c][:].rearrange("v (u e p) -> v u p e", u=2, e=2))
                words = zr[:].bitcast(F32)
                for u in range(2):
                    slot = 2 * c2 + u
                    nc.tensor.transpose(back[:, slot * P : (slot + 1) * P], words[:, u * P : (u + 1) * P], ident[:])
            nc.scalar.copy(
                z5[:, 4 - pair, :].rearrange("p (c v u) -> p c v u", c=2, u=2),
                back[:].rearrange("p (c u v) -> p c v u", c=2, u=2),
            )
        z2w = keep.tile([P, V], U32, name="z2w", align_bytes=64)
        z2s = keep.tile([P, V], U8, name="z2s", align_bytes=64)
        for pair in range(2):
            cols = slice(pair * 256, (pair + 1) * 256)
            nc.vector.quantize_mx(out=z2w[:, cols].bitcast(FP8X4), scales=z2s[:, cols], in_=z5[:, 4 - pair, :].bitcast(BF16))
        a_sub(3)

        z_v = z.rearrange("p h (g t u) -> p t g h u", t=4, u=4)
        zbs = []
        for t in range(4):
            zb = keep.tile([P, N], BF16, name=f"zb{t}", align_bytes=64)
            zbs.append(zb)

        def z_round(t):
            dst = zbs[t][:].rearrange("p (g u h) -> p g h u", u=4, h=4)
            if t in (1, 2):
                nc.scalar.copy(dst, z_v[:, t])
            else:
                nc.vector.tensor_copy(dst, z_v[:, t])

        def s_front(t):
            zw = keep.tile([P, P], U32, name=f"zw{t}", align_bytes=64)
            zs = keep.tile([P, P], U8, name=f"zs{t}", align_bytes=64)
            nc.vector.quantize_mx(out=zw[:].bitcast(FP8X4), scales=zs[:], in_=zbs[t][:])
            acc = psum.tile([P, N], F32, name="acc", bufs=4)
            mx(acc[:], zw[:], zs[:], z2w[:], z2s[:])
            nc.scalar.activation(wins[t][:, 0:N], acc[:], ACT.Copy, scale=0.0625)
            sg = ring.tile([P, N], F32, name="sg")
            nc.scalar.activation(sg[:], wins[t][:].indirect(l_n6[:]), ACT.Sigmoid)
            state["s", t] = sg

        z_round(0)
        z_round(1)
        z_round(2)
        z_round(3)
        for t in range(4):
            s_front(t)

        out_v = out.rearrange("(g t u) v -> t g u v", t=4, u=4)

        def s_fetch(t):
            g7 = ring.tile([P, N], F32, name="g7")
            nc.vector.tensor_copy(g7[:], wins[t][:].indirect(l_n7[:]))
            state["g", t] = g7

        s_fetch(0)
        for t in range(4):
            m = ring.tile([P, N], F32, name="m")
            o = wins[(t + 1) % 4][:, N:WIN]
            parts = [slice(0, N)] if t < 3 else [slice(0, N // 2), slice(N // 2, N)]
            for cols in parts:
                nc.vector.tensor_tensor(m[:, cols], wins[t][:, cols], state["s", t][:, cols], ALU.mult)
            if t < 3:
                s_fetch(t + 1)
            for cols in parts:
                nc.vector.tensor_tensor(o[:, cols], m[:, cols], state["g", t][:, cols], ALU.max)
                nc.sync.dma_start(out_v[t][:, :, cols], o[:, cols])
